import numpy as np
import ml_dtypes


def mxq(x, axis, fmt="e4m3"):
    dtype, down = {"e4m3": (ml_dtypes.float8_e4m3fn, 7), "e5m2": (ml_dtypes.float8_e5m2, 14)}[fmt]
    v = np.moveaxis(np.asarray(x, np.float32).astype(ml_dtypes.bfloat16).astype(np.float64), axis, -1)
    blocks = v.reshape(v.shape[:-1] + (-1, 32))
    amax = np.abs(blocks).max(-1, keepdims=True)
    byte = np.maximum(np.where(amax > 0, np.frexp(amax)[1] - 1 + 127, 0) - down, 1)
    scale = np.exp2(byte - 127.0)
    codes = (blocks / scale).astype(np.float32).astype(dtype).astype(np.float64)
    return np.moveaxis((codes * scale).reshape(v.shape), -1, axis)


WIDE = False


def mx_kscale(k):
    if not WIDE:
        return np.ones(k)
    levels = np.array([10, -10, 5, -5, 0])
    if k % 512:
        return np.exp2(np.random.permutation(np.resize(levels, k // 32))).repeat(32)
    a = np.empty((k // 512, 16))
    for p in range(k // 512):
        a[p, :8] = np.random.permutation(np.resize(levels, 8))
        for g in range(8):
            far = levels[np.abs(levels - a[p, g]) >= 10]
            a[p, g + 8] = far[np.random.randint(len(far))]
    return np.exp2(a.ravel()).repeat(32)


def f64(x):
    return np.asarray(x).astype(np.float64)


def striped(idx):
    return np.tile(np.asarray(idx).reshape(-1, 16).T, (8, 1)).astype(np.uint16)


def unstriped(offs):
    return offs[:16].T.reshape(-1).astype(np.int64)


E2M1 = np.array([0.0, 0.5, 1.0, 1.5, 2.0, 3.0, 4.0, 6.0, -0.0, -0.5, -1.0, -1.5, -2.0, -3.0, -4.0, -6.0])


def pack_weight(w, fmt):
    k, n = w.shape
    w = f64(np.asarray(w, np.float32).astype(ml_dtypes.bfloat16)).reshape(k // 32, 32, n)
    amax = np.abs(w).max(1)
    if fmt == "e4m3":
        byte = np.frexp(amax)[1] - 1 + 127 - 7
    else:
        mant, ex = np.frexp(amax / 6.0)
        byte = np.where(mant > 0.5, ex, ex - 1) + 127
    byte = np.clip(np.where(amax > 0, byte, 1), 1, 254)
    scaled = (w * np.exp2(127.0 - byte)[:, None, :]).reshape(k, n).astype(np.float32)
    by_word = np.ascontiguousarray(scaled.reshape(k // 512, 128, 4, n).transpose(0, 1, 3, 2))
    if fmt == "e4m3":
        words = by_word.astype(ml_dtypes.float8_e4m3fn).view(np.uint8)
    else:
        c = by_word.astype(ml_dtypes.float4_e2m1fn).view(np.uint8) & 0xF
        words = (c[..., 0::2] | (c[..., 1::2] << 4)).reshape(k // 512, 128, 2 * n)
    return np.ascontiguousarray(words), np.ascontiguousarray(byte.astype(np.uint8).reshape(k // 512, 16, n))


def unpack_weight(words, scales, fmt):
    g, _, n = scales.shape
    words = np.ascontiguousarray(words).reshape(g, 128, n, -1)
    if fmt == "e4m3":
        vals = words.view(ml_dtypes.float8_e4m3fn).astype(np.float64)
    else:
        nib = np.empty((g, 128, n, 4), np.uint8)
        nib[..., 0::2] = words & 0xF
        nib[..., 1::2] = words >> 4
        vals = E2M1[nib]
    vals = vals * np.repeat(np.exp2(scales.astype(np.float64) - 127.0), 8, axis=1)[..., None]
    return vals.transpose(0, 1, 3, 2).reshape(g * 512, n)


def bf(x):
    return np.asarray(x, np.float32).astype(ml_dtypes.bfloat16)


def planes(Y):
    r, m = Y.shape
    b = f64(bf(Y)).reshape(r // 32, 32, m)
    amax = np.abs(b).max(1)
    byte = np.clip(np.where(amax > 0, np.frexp(amax)[1] - 1 + 127 - 7, 1), 1, 254)
    codes = (b * np.exp2(127.0 - byte)[:, None, :]).reshape(r, m).astype(np.float32).astype(ml_dtypes.float8_e4m3fn).view(np.uint8)
    words = codes.reshape(r // 512, 128, 4, m).transpose(0, 1, 3, 2)
    return np.ascontiguousarray(words), np.ascontiguousarray(byte.astype(np.uint8).reshape(r // 512, 16, m))


D, E, T, I, Q = 512, 512, 2048, 512, 256


def setup_inputs():
    n = np.random.standard_normal
    idx = np.random.permutation(T)[:I]
    fd = mx_kscale(D)
    fi = mx_kscale(I)
    ti = np.ones(T)
    ti[idx] = fi
    keysp = pack_weight(n((D, T)) / fd[:, None], "e4m3")
    return {
        "query": (n((D, Q)) * 0.4 / np.sqrt(D) * fd[:, None]).astype(np.float32),
        "keys_words": keysp[0],
        "keys_scales": keysp[1],
        "gain": (np.random.uniform(0.3, 0.8, (Q, 1))).astype(np.float32),
        "os": (np.random.uniform(4.0, 16.0, (1, I)) * fi).astype(np.float32),
        "vals": (n((E, T)) / ti).astype(np.float32),
        "offs": striped(idx),
    }


def reference(query, keys_words, keys_scales, gain, os, vals, offs):
    idx = unstriped(offs)
    keysu = unpack_weight(keys_words, keys_scales, "e4m3")
    queryq = mxq(f64(query), 0, "e4m3")
    keysidxg = keysu[:, idx]
    a = queryq.T @ keysidxg
    p = np.exp(a - np.max(a, axis=1, keepdims=True))
    z = np.sum(p, axis=1, keepdims=True)
    u1 = p / z * f64(gain) * 512.0
    p2 = np.exp(u1 - np.max(u1, axis=1, keepdims=True))
    z2 = np.sum(p2, axis=1, keepdims=True)
    w = p2 / z2
    wo1 = w * f64(os)
    wt1 = wo1.T
    vt1 = f64(vals)[:, idx].T
    vt1q = mxq(vt1, 0, "e4m3")
    wt1q = mxq(wt1, 0, "e4m3")
    o = vt1q.T @ wt1q
    words, scales = planes(o)
    return o, words, scales

@@ -1,0 +1,214 @@
+from contextlib import ExitStack
+
+import concourse.mybir as mybir
+from concourse.masks import make_identity
+
+D, E, T, I, Q = 512, 512, 2048, 512, 256
+FLOPS = 2 * D * I * Q + 2 * I * E * Q
+
+F32 = mybir.dt.float32
+BF16 = mybir.dt.bfloat16
+I32 = mybir.dt.int32
+U32 = mybir.dt.uint32
+U16 = mybir.dt.uint16
+U8 = mybir.dt.uint8
+FP8X4 = mybir.dt.float8_e4m3fn_x4
+ALU = mybir.AluOpType
+ACT = mybir.ActivationFunctionType
+AXIS = mybir.AxisListType
+
+P = 128
+PACK = 4
+HALVES = Q // P
+
+
+def tile_attend_doubled_pl_kernel(tc, query, keys_words, keys_scales, gain, slot_factor, vals, offs, out_0, out_1, out_2):
+    nc = tc.nc
+    with ExitStack() as ctx:
+        sb = ctx.enter_context(tc.tile_pool(name="sb", bufs=1))
+        ps = ctx.enter_context(tc.psum_pool(name="ps", bufs=1))
+
+        offsets = sb.tile([P, I // 16], U16, name="offsets")
+        nc.sync.dma_start(offsets[:], offs)
+
+        key_bytes = sb.tile([P, T], U8, name="key_bytes", align_bytes=64)
+        nc.vector.memset(key_bytes[:].bitcast(I32), 0)
+        for quad in range(4):
+            nc.scalar.dma_start(
+                key_bytes[32 * quad : 32 * quad + 4, :].bitcast(I32),
+                keys_scales[0, 4 * quad : 4 * quad + 4, :].bitcast(I32),
+            )
+
+        q_raw = sb.tile([P, PACK, Q], F32, name="q_raw")
+        nc.sync.dma_start(q_raw[:], query.rearrange("(p t) q -> p t q", t=PACK))
+        key_words = sb.tile([P, T], U32, name="key_words", align_bytes=64)
+        nc.sync.dma_start(key_words[:].bitcast(I32), keys_words[0].rearrange("p n t -> p (n t)").bitcast(I32))
+
+        vals_rows = vals.rearrange("(p t) c -> t p c", t=PACK)
+        v_pool = [sb.tile([P, T], F32, name="v_pool%d" % t) for t in range(PACK)]
+        nc.sync.dma_start(v_pool[0][:], vals_rows[0])
+        gain_col = sb.tile([P, HALVES], F32, name="gain_col")
+        with nc.allow_non_contiguous_dma(reason="one gain value to a partition"):
+            nc.sync.dma_start(gain_col[:], gain.rearrange("(h p) o -> p (h o)", p=P))
+        os_col = sb.tile([P, PACK], F32, name="os_col")
+        nc.sync.dma_start(os_col[:], slot_factor.rearrange("o (p t) -> p (o t)", t=PACK))
+        for t in range(1, PACK):
+            nc.sync.dma_start(v_pool[t][:], vals_rows[t])
+
+        ident = sb.tile([P, P], F32, name="ident")
+        make_identity(nc, ident[:])
+
+        warm = sb.tile([P, 1], F32, name="warm")
+        nc.scalar.activation(warm[:], ident[:, 0:1], ACT.Exp)
+
+        q_bf = sb.tile([P, Q, PACK], BF16, name="q_bf", align_bytes=64)
+        nc.vector.tensor_copy(
+            q_bf[:].rearrange("p (c i) t -> p c t i", i=4),
+            q_raw[:].rearrange("p t (c i) -> p c t i", i=4),
+        )
+        kg_bytes = sb.tile([P, I], U8, name="kg_bytes", align_bytes=64)
+        nc.vector.tensor_copy(kg_bytes[:], key_bytes[:].indirect(offsets[:]))
+        q_codes = sb.tile([P, Q], U32, name="q_codes", align_bytes=64)
+        q_scales = sb.tile([P, Q], U8, name="q_scales", align_bytes=64)
+        nc.vector.quantize_mx(q_codes[:].bitcast(FP8X4), q_scales[:], q_bf[:].rearrange("p q t -> p (q t)"))
+
+        kg_words = sb.tile([P, I], U32, name="kg_words", align_bytes=64)
+        nc.vector.tensor_copy(kg_words[:], key_words[:].indirect(offsets[:]))
+
+        scores = [ps.tile([P, I], F32, name="scores%d" % h, tag="half%d" % h) for h in range(HALVES)]
+        for h in range(HALVES):
+            cols = slice(h * P, (h + 1) * P)
+            nc.tensor.matmul_mx(
+                scores[h][:],
+                lhsT=q_codes[:, cols].bitcast(FP8X4),
+                lhsT_scale=q_scales[:, cols],
+                rhs=kg_words[:].bitcast(FP8X4),
+                rhs_scale=kg_bytes[:],
+                start=True,
+                stop=True,
+            )
+
+        gain512 = sb.tile([P, HALVES], F32, name="gain512")
+        nc.vector.tensor_scalar(gain512[:], gain_col[:], float(I), None, ALU.mult)
+        os_rows = ps.tile([P, PACK, P], F32, name="os_rows")
+        for t in range(PACK):
+            nc.tensor.transpose(os_rows[:, t, :], os_col[:, t : t + 1].to_broadcast([P, P]), ident[:])
+
+        def col(name):
+            return sb.tile([P, 1], F32, name=name)
+
+        v_codes, v_scales = [], []
+
+        def values(t):
+            picked = sb.tile([P, I], BF16, name="picked%d" % t, align_bytes=64)
+            nc.vector.tensor_copy(picked[:], v_pool[t][:].indirect(offsets[:]))
+            turned = ps.tile([P, 2, P], F32, name="v_turned%d" % t, tag="v_turned", bufs=2)
+            words = picked[:].bitcast(F32)
+            for u in range(2):
+                nc.tensor.transpose(turned[:, u, :], words[:, u : I // 2 : 2], ident[:])
+            v_bf = sb.tile([P, P * PACK], BF16, name="v_bf%d" % t, align_bytes=64)
+            nc.scalar.copy(
+                v_bf[:].bitcast(F32).rearrange("p (m u) -> p m u", u=2),
+                turned[:].rearrange("p u m -> p m u"),
+            )
+            codes = sb.tile([P, P], U32, name="v_codes%d" % t, align_bytes=64)
+            scales = sb.tile([P, P], U8, name="v_scales%d" % t, align_bytes=64)
+            nc.vector.quantize_mx(codes[:].bitcast(FP8X4), scales[:], v_bf[:])
+            v_codes.append(codes)
+            v_scales.append(scales)
+
+        neg_max, p1, z1, pu, top, rz1, bias2, p2, z2, rz2, w_bf = [[] for k in range(11)]
+        for h in range(HALVES):
+            neg_max.append(col("neg_max%d" % h))
+            nc.vector.tensor_reduce(neg_max[h][:], scores[h][:], AXIS.X, ALU.max, negate=True)
+            p1.append(sb.tile([P, I], F32, name="p1_%d" % h))
+            z1.append(col("z1_%d" % h))
+            nc.scalar.activation(p1[h][:], scores[h][:], ACT.Exp, bias=neg_max[h][:], accum_out=z1[h][:])
+        values(0)
+        for h in range(HALVES):
+            pu.append(sb.tile([P, I], F32, name="pu%d" % h))
+            top.append(col("top%d" % h))
+            rz1.append(col("rz1_%d" % h))
+            bias2.append(col("bias2_%d" % h))
+            nc.vector.reciprocal(rz1[h][:], z1[h][:])
+            nc.vector.tensor_scalar(pu[h][:], p1[h][:], gain512[:, h : h + 1], None, ALU.mult, ALU.max, accum_out=top[h][:])
+        for h in range(HALVES):
+            nc.vector.tensor_scalar(bias2[h][:], top[h][:], rz1[h][:], -1.0, ALU.mult, ALU.mult)
+            p2.append(sb.tile([P, I], F32, name="p2_%d" % h))
+            z2.append(col("z2_%d" % h))
+            nc.scalar.activation(p2[h][:], pu[h][:], ACT.Exp, bias=bias2[h][:], scale=rz1[h][:], accum_out=z2[h][:])
+        values(1)
+        w_codes, w_scales = [], []
+        for h in range(HALVES):
+            rz2.append(col("rz2_%d" % h))
+            nc.vector.reciprocal(rz2[h][:], z2[h][:])
+        for h in range(HALVES):
+            w_bf.append(sb.tile([P, I], BF16, name="w_bf%d" % h, align_bytes=64))
+            nc.vector.scalar_tensor_tensor(
+                w_bf[h][:].rearrange("q (p t) -> q p t", t=PACK),
+                p2[h][:].rearrange("q (p t) -> q p t", t=PACK),
+                rz2[h][:],
+                os_rows[:].rearrange("q t p -> q p t"),
+                ALU.mult,
+                ALU.mult,
+            )
+            turned = ps.tile([P, 2, P], F32, name="w_turned%d" % h, tag="half%d" % h)
+            words = w_bf[h][:].bitcast(F32)
+            for u in range(2):
+                nc.tensor.transpose(turned[:, u, :], words[:, u : I // 2 : 2], ident[:])
+            wt_bf = sb.tile([P, P * PACK], BF16, name="wt_bf%d" % h, align_bytes=64)
+            nc.scalar.copy(
+                wt_bf[:].bitcast(F32).rearrange("p (m u) -> p m u", u=2),
+                turned[:].rearrange("p u m -> p m u"),
+            )
+            codes = sb.tile([P, P], U32, name="w_codes%d" % h, align_bytes=64)
+            scales = sb.tile([P, P], U8, name="w_scales%d" % h, align_bytes=64)
+            nc.vector.quantize_mx(codes[:].bitcast(FP8X4), scales[:], wt_bf[:])
+            w_codes.append(codes)
+            w_scales.append(scales)
+        values(2)
+
+        sums = [ps.tile([P, PACK, P], F32, name="sums%d" % h) for h in range(HALVES)]
+        result = sb.tile([P, PACK, Q], F32, name="result")
+        out_rows = out_0.rearrange("(p t) q -> p t q", t=PACK)
+
+        def product(t, h):
+            nc.tensor.matmul_mx(
+                sums[h][:, t, :],
+                lhsT=v_codes[t][:].bitcast(FP8X4),
+                lhsT_scale=v_scales[t][:],
+                rhs=w_codes[h][:].bitcast(FP8X4),
+                rhs_scale=w_scales[h][:],
+                start=True,
+                stop=True,
+            )
+
+        last = PACK - 1
+        for h in range(HALVES):
+            for t in range(last):
+                product(t, h)
+            nc.scalar.copy(result[:, 0:last, h * P : (h + 1) * P], sums[h][:, 0:last, :])
+        nc.sync.dma_start(out_rows[:, 0:last, :], result[:, 0:last, :])
+
+        values(last)
+        for h in range(HALVES):
+            product(last, h)
+        y_bf = [sb.tile([P, P, PACK], BF16, name="y_bf%d" % h, align_bytes=64) for h in range(HALVES)]
+        nc.vector.tensor_copy(y_bf[0][:], sums[0][:].rearrange("p t q -> p q t"))
+        nc.scalar.copy(y_bf[1][:], sums[1][:].rearrange("p t q -> p q t"))
+        y_codes = sb.tile([P, Q], U32, name="y_codes", align_bytes=64)
+        y_scales = sb.tile([P, Q], U8, name="y_scales", align_bytes=64)
+        for h in (1, 0):
+            cols = slice(h * P, (h + 1) * P)
+            nc.vector.quantize_mx(
+                y_codes[:, cols].bitcast(FP8X4), y_scales[:, cols], y_bf[h][:].rearrange("p q t -> p (q t)")
+            )
+            nc.scalar.copy(result[:, last, cols], sums[h][:, last, :])
+        nc.scalar.dma_start(out_rows[:, last, :], result[:, last, :])
+        nc.sync.dma_start(out_1[0].rearrange("p n t -> p (n t)").bitcast(I32), y_codes[:].bitcast(I32))
+        for quad in range(4):
+            queue = nc.sync if quad < 2 else nc.scalar
+            queue.dma_start(
+                out_2[0, 4 * quad : 4 * quad + 4, :].bitcast(I32),
+                y_scales[32 * quad : 32 * quad + 4, :].bitcast(I32),
+            )

@@ -28,38 +28,37 @@ def tile_attend_doubled_pl_kernel(tc, query, keys_words, keys_scales, gain, slot
         sb = ctx.enter_context(tc.tile_pool(name="sb", bufs=1))
         ps = ctx.enter_context(tc.psum_pool(name="ps", bufs=1))
 
+        q_raw = sb.tile([P, PACK, Q], F32, name="q_raw")
+        nc.sync.dma_start(q_raw[:], query.rearrange("(p t) q -> p t q", t=PACK))
         offsets = sb.tile([P, I // 16], U16, name="offsets")
         nc.sync.dma_start(offsets[:], offs)
 
         key_bytes = sb.tile([P, T], U8, name="key_bytes", align_bytes=64)
-        nc.vector.memset(key_bytes[:].bitcast(I32), 0)
+        nc.gpsimd.memset(key_bytes[:].bitcast(I32), 0)
         for quad in range(4):
-            nc.scalar.dma_start(
+            nc.sync.dma_start(
                 key_bytes[32 * quad : 32 * quad + 4, :].bitcast(I32),
                 keys_scales[0, 4 * quad : 4 * quad + 4, :].bitcast(I32),
             )
-
-        q_raw = sb.tile([P, PACK, Q], F32, name="q_raw")
-        nc.sync.dma_start(q_raw[:], query.rearrange("(p t) q -> p t q", t=PACK))
         key_words = sb.tile([P, T], U32, name="key_words", align_bytes=64)
         nc.sync.dma_start(key_words[:].bitcast(I32), keys_words[0].rearrange("p n t -> p (n t)").bitcast(I32))
-
-        vals_rows = vals.rearrange("(p t) c -> t p c", t=PACK)
-        v_pool = [sb.tile([P, T], F32, name="v_pool%d" % t) for t in range(PACK)]
-        nc.sync.dma_start(v_pool[0][:], vals_rows[0])
         gain_col = sb.tile([P, HALVES], F32, name="gain_col")
         with nc.allow_non_contiguous_dma(reason="one gain value to a partition"):
             nc.sync.dma_start(gain_col[:], gain.rearrange("(h p) o -> p (h o)", p=P))
         os_col = sb.tile([P, PACK], F32, name="os_col")
         nc.sync.dma_start(os_col[:], slot_factor.rearrange("o (p t) -> p (o t)", t=PACK))
-        for t in range(1, PACK):
+
+        vals_rows = vals.rearrange("(p t) c -> t p c", t=PACK)
+        v_pool = [sb.tile([P, T], F32, name="v_pool%d" % t, tag="pool%d" % t, align_bytes=64) for t in range(PACK)]
+        for t in range(PACK):
             nc.sync.dma_start(v_pool[t][:], vals_rows[t])
 
         ident = sb.tile([P, P], F32, name="ident")
         make_identity(nc, ident[:])
+        os_rows = ps.tile([P, PACK, P], F32, name="os_rows")
+        for t in range(PACK):
+            nc.tensor.transpose(os_rows[:, t, :], os_col[:, t : t + 1].to_broadcast([P, P]), ident[:])
 
-        warm = sb.tile([P, 1], F32, name="warm")
-        nc.scalar.activation(warm[:], ident[:, 0:1], ACT.Exp)
 
         q_bf = sb.tile([P, Q, PACK], BF16, name="q_bf", align_bytes=64)
         nc.vector.tensor_copy(
@@ -73,138 +72,140 @@ def tile_attend_doubled_pl_kernel(tc, query, keys_words, keys_scales, gain, slot
         nc.vector.quantize_mx(q_codes[:].bitcast(FP8X4), q_scales[:], q_bf[:].rearrange("p q t -> p (q t)"))
 
         kg_words = sb.tile([P, I], U32, name="kg_words", align_bytes=64)
-        nc.vector.tensor_copy(kg_words[:], key_words[:].indirect(offsets[:]))
-
         scores = [ps.tile([P, I], F32, name="scores%d" % h, tag="half%d" % h) for h in range(HALVES)]
-        for h in range(HALVES):
-            cols = slice(h * P, (h + 1) * P)
-            nc.tensor.matmul_mx(
-                scores[h][:],
-                lhsT=q_codes[:, cols].bitcast(FP8X4),
-                lhsT_scale=q_scales[:, cols],
-                rhs=kg_words[:].bitcast(FP8X4),
-                rhs_scale=kg_bytes[:],
-                start=True,
-                stop=True,
-            )
-
-        gain512 = sb.tile([P, HALVES], F32, name="gain512")
-        nc.vector.tensor_scalar(gain512[:], gain_col[:], float(I), None, ALU.mult)
-        os_rows = ps.tile([P, PACK, P], F32, name="os_rows")
-        for t in range(PACK):
-            nc.tensor.transpose(os_rows[:, t, :], os_col[:, t : t + 1].to_broadcast([P, P]), ident[:])
+        for part in range(2):
+            slots = slice(part * I // 2, (part + 1) * I // 2)
+            entries = offsets[:, part * I // 32 : (part + 1) * I // 32]
+            nc.vector.tensor_copy(kg_words[:, slots], key_words[:].indirect(entries))
+            for h in range(HALVES):
+                cols = slice(h * P, (h + 1) * P)
+                nc.tensor.matmul_mx(
+                    scores[h][:, slots],
+                    lhsT=q_codes[:, cols].bitcast(FP8X4),
+                    lhsT_scale=q_scales[:, cols],
+                    rhs=kg_words[:, slots].bitcast(FP8X4),
+                    rhs_scale=kg_bytes[:, slots],
+                    start=True,
+                    stop=True,
+                )
 
         def col(name):
             return sb.tile([P, 1], F32, name=name)
 
-        v_codes, v_scales = [], []
-
-        def values(t):
-            picked = sb.tile([P, I], BF16, name="picked%d" % t, align_bytes=64)
-            nc.vector.tensor_copy(picked[:], v_pool[t][:].indirect(offsets[:]))
-            turned = ps.tile([P, 2, P], F32, name="v_turned%d" % t, tag="v_turned", bufs=2)
-            words = picked[:].bitcast(F32)
+        def turn(rows_bf, name, bank_tag, bank_bufs):
+            turned = ps.tile([P, 2, P], F32, name=name + "_turned", tag=bank_tag, bufs=bank_bufs)
+            words = rows_bf[:].bitcast(F32)
             for u in range(2):
                 nc.tensor.transpose(turned[:, u, :], words[:, u : I // 2 : 2], ident[:])
-            v_bf = sb.tile([P, P * PACK], BF16, name="v_bf%d" % t, align_bytes=64)
+            grouped = sb.tile([P, P * PACK], BF16, name=name + "_grouped", align_bytes=64)
             nc.scalar.copy(
-                v_bf[:].bitcast(F32).rearrange("p (m u) -> p m u", u=2),
+                grouped[:].bitcast(F32).rearrange("p (m u) -> p m u", u=2),
                 turned[:].rearrange("p u m -> p m u"),
             )
-            codes = sb.tile([P, P], U32, name="v_codes%d" % t, align_bytes=64)
-            scales = sb.tile([P, P], U8, name="v_scales%d" % t, align_bytes=64)
-            nc.vector.quantize_mx(codes[:].bitcast(FP8X4), scales[:], v_bf[:])
-            v_codes.append(codes)
-            v_scales.append(scales)
+            return grouped
 
-        neg_max, p1, z1, pu, top, rz1, bias2, p2, z2, rz2, w_bf = [[] for k in range(11)]
+        def quantize(grouped, name, codes):
+            scales = sb.tile([P, P], U8, name=name + "_scales", align_bytes=64)
+            nc.vector.quantize_mx(codes.bitcast(FP8X4), scales[:], grouped[:])
+            return codes, scales[:]
+
+        def codes_tile(name, count, tag):
+            return sb.tile([P, count * P], U32, name=name, tag=tag, align_bytes=64)
+
+        def pick_values(t):
+            picked = sb.tile([P, I], BF16, name="picked%d" % t, align_bytes=64)
+            nc.vector.tensor_copy(picked[:], v_pool[t][:].indirect(offsets[:]))
+            return turn(picked, "v%d" % t, "v_turned", 2)
+
+        neg_max, p1, top, bias2, p2, z2, w_grouped = [[] for k in range(7)]
+        z1 = sb.tile([P, HALVES], F32, name="z1")
         for h in range(HALVES):
             neg_max.append(col("neg_max%d" % h))
             nc.vector.tensor_reduce(neg_max[h][:], scores[h][:], AXIS.X, ALU.max, negate=True)
             p1.append(sb.tile([P, I], F32, name="p1_%d" % h))
-            z1.append(col("z1_%d" % h))
-            nc.scalar.activation(p1[h][:], scores[h][:], ACT.Exp, bias=neg_max[h][:], accum_out=z1[h][:])
-        values(0)
+            nc.scalar.activation(p1[h][:], scores[h][:], ACT.Exp, bias=neg_max[h][:], accum_out=z1[:, h : h + 1])
+            top.append(sb.tile([P, 2], F32, name="top%d" % h))
+            nc.vector.memset(top[h][:, 0:1], -1.0)
+        v_grouped = [pick_values(0)]
+        gained = sb.tile([P, HALVES * (I + 1)], F32, name="gained", tag="pool0", align_bytes=64)
+        pu = [gained[:, h * I : (h + 1) * I] for h in range(HALVES)]
+        rz1 = [gained[:, HALVES * I + h : HALVES * I + h + 1] for h in range(HALVES)]
         for h in range(HALVES):
-            pu.append(sb.tile([P, I], F32, name="pu%d" % h))
-            top.append(col("top%d" % h))
-            rz1.append(col("rz1_%d" % h))
-            bias2.append(col("bias2_%d" % h))
-            nc.vector.reciprocal(rz1[h][:], z1[h][:])
-            nc.vector.tensor_scalar(pu[h][:], p1[h][:], gain512[:, h : h + 1], None, ALU.mult, ALU.max, accum_out=top[h][:])
-        for h in range(HALVES):
-            nc.vector.tensor_scalar(bias2[h][:], top[h][:], rz1[h][:], -1.0, ALU.mult, ALU.mult)
+            nc.vector.tensor_scalar(pu[h], p1[h][:], gain_col[:, h : h + 1], None, ALU.mult, ALU.max, accum_out=top[h][:, 1:2])
+            if h == 0:
+                nc.vector.reciprocal(gained[:, HALVES * I :], z1[:])
+            bias2.append(sb.tile([P, 2], F32, name="bias2_%d" % h))
+            nc.vector.tensor_scalar(bias2[h][:], top[h][:], rz1[h], -float(I), ALU.mult, ALU.mult)
             p2.append(sb.tile([P, I], F32, name="p2_%d" % h))
             z2.append(col("z2_%d" % h))
-            nc.scalar.activation(p2[h][:], pu[h][:], ACT.Exp, bias=bias2[h][:], scale=rz1[h][:], accum_out=z2[h][:])
-        values(1)
-        w_codes, w_scales = [], []
+            nc.scalar.activation(p2[h][:], pu[h], ACT.Exp, bias=bias2[h][:, 1:2], scale=bias2[h][:, 0:1], accum_out=z2[h][:])
+        v_mx = [quantize(v_grouped[0], "v0", codes_tile("v0_codes", 1, "v0_codes")[:])]
+        v_grouped.append(pick_values(1))
+        rz2 = sb.tile([P, HALVES], F32, name="rz2", tag="pool1", align_bytes=64)
         for h in range(HALVES):
-            rz2.append(col("rz2_%d" % h))
-            nc.vector.reciprocal(rz2[h][:], z2[h][:])
+            nc.vector.reciprocal(rz2[:, h : h + 1], z2[h][:])
         for h in range(HALVES):
-            w_bf.append(sb.tile([P, I], BF16, name="w_bf%d" % h, align_bytes=64))
+            w_bf = sb.tile([P, I], BF16, name="w_bf%d" % h, align_bytes=64)
             nc.vector.scalar_tensor_tensor(
-                w_bf[h][:].rearrange("q (p t) -> q p t", t=PACK),
+                w_bf[:].rearrange("q (p t) -> q p t", t=PACK),
                 p2[h][:].rearrange("q (p t) -> q p t", t=PACK),
-                rz2[h][:],
+                rz2[:, h : h + 1],
                 os_rows[:].rearrange("q t p -> q p t"),
                 ALU.mult,
                 ALU.mult,
             )
-            turned = ps.tile([P, 2, P], F32, name="w_turned%d" % h, tag="half%d" % h)
-            words = w_bf[h][:].bitcast(F32)
-            for u in range(2):
-                nc.tensor.transpose(turned[:, u, :], words[:, u : I // 2 : 2], ident[:])
-            wt_bf = sb.tile([P, P * PACK], BF16, name="wt_bf%d" % h, align_bytes=64)
-            nc.scalar.copy(
-                wt_bf[:].bitcast(F32).rearrange("p (m u) -> p m u", u=2),
-                turned[:].rearrange("p u m -> p m u"),
-            )
-            codes = sb.tile([P, P], U32, name="w_codes%d" % h, align_bytes=64)
-            scales = sb.tile([P, P], U8, name="w_scales%d" % h, align_bytes=64)
-            nc.vector.quantize_mx(codes[:].bitcast(FP8X4), scales[:], wt_bf[:])
-            w_codes.append(codes)
-            w_scales.append(scales)
-        values(2)
+            w_grouped.append(turn(w_bf, "w%d" % h, "half%d" % h, 1))
+        v_grouped.append(pick_values(2))
+        mid_codes = codes_tile("mid_codes", 3, "pool2")
+        v_mx.append(quantize(v_grouped[1], "v1", mid_codes[:, 0:P]))
+        w_mx = [quantize(w_grouped[h], "w%d" % h, mid_codes[:, (h + 1) * P : (h + 2) * P]) for h in range(HALVES)]
 
         sums = [ps.tile([P, PACK, P], F32, name="sums%d" % h) for h in range(HALVES)]
         result = sb.tile([P, PACK, Q], F32, name="result")
         out_rows = out_0.rearrange("(p t) q -> p t q", t=PACK)
 
-        def product(t, h):
-            nc.tensor.matmul_mx(
-                sums[h][:, t, :],
-                lhsT=v_codes[t][:].bitcast(FP8X4),
-                lhsT_scale=v_scales[t][:],
-                rhs=w_codes[h][:].bitcast(FP8X4),
-                rhs_scale=w_scales[h][:],
-                start=True,
-                stop=True,
-            )
+        def products(t):
+            for h in range(HALVES):
+                nc.tensor.matmul_mx(
+                    sums[h][:, t, :],
+                    lhsT=v_mx[t][0].bitcast(FP8X4),
+                    lhsT_scale=v_mx[t][1],
+                    rhs=w_mx[h][0].bitcast(FP8X4),
+                    rhs_scale=w_mx[h][1],
+                    start=True,
+                    stop=True,
+                )
 
-        last = PACK - 1
-        for h in range(HALVES):
-            for t in range(last):
-                product(t, h)
-            nc.scalar.copy(result[:, 0:last, h * P : (h + 1) * P], sums[h][:, 0:last, :])
-        nc.sync.dma_start(out_rows[:, 0:last, :], result[:, 0:last, :])
+        def hand_out(rows, h):
+            nc.scalar.copy(result[:, rows, h * P : (h + 1) * P], sums[h][:, rows, :])
 
-        values(last)
+        products(0)
+        products(1)
         for h in range(HALVES):
-            product(last, h)
+            hand_out(slice(0, 2), h)
+        nc.sync.dma_start(out_rows[:, 0:2, :], result[:, 0:2, :])
+        v_grouped.append(pick_values(3))
+        v_mx.append(quantize(v_grouped[2], "v2", codes_tile("v2_codes", 1, "pool3")[:]))
+        products(2)
+        for h in range(HALVES):
+            hand_out(2, h)
+        nc.sync.dma_start(out_rows[:, 2, :], result[:, 2, :])
+        v_mx.append(quantize(v_grouped[3], "v3", codes_tile("v3_codes", 1, "v3_codes")[:]))
+        products(3)
+
         y_bf = [sb.tile([P, P, PACK], BF16, name="y_bf%d" % h, align_bytes=64) for h in range(HALVES)]
-        nc.vector.tensor_copy(y_bf[0][:], sums[0][:].rearrange("p t q -> p q t"))
-        nc.scalar.copy(y_bf[1][:], sums[1][:].rearrange("p t q -> p q t"))
+        nc.scalar.copy(y_bf[0][:], sums[0][:].rearrange("p t q -> p q t"))
+        nc.vector.tensor_copy(y_bf[1][:], sums[1][:].rearrange("p t q -> p q t"))
+        for h in range(HALVES):
+            hand_out(3, h)
+        nc.scalar.dma_start(out_rows[:, 3, :], result[:, 3, :])
         y_codes = sb.tile([P, Q], U32, name="y_codes", align_bytes=64)
         y_scales = sb.tile([P, Q], U8, name="y_scales", align_bytes=64)
-        for h in (1, 0):
+        for h in range(HALVES):
             cols = slice(h * P, (h + 1) * P)
             nc.vector.quantize_mx(
                 y_codes[:, cols].bitcast(FP8X4), y_scales[:, cols], y_bf[h][:].rearrange("p q t -> p (q t)")
             )
-            nc.scalar.copy(result[:, last, cols], sums[h][:, last, :])
-        nc.scalar.dma_start(out_rows[:, last, :], result[:, last, :])
         nc.sync.dma_start(out_1[0].rearrange("p n t -> p (n t)").bitcast(I32), y_codes[:].bitcast(I32))
         for quad in range(4):
             queue = nc.sync if quad < 2 else nc.scalar

@@ -20,12 +20,14 @@ AXIS = mybir.AxisListType
 P = 128
 PACK = 4
 HALVES = Q // P
+POOL_BYTES = 4 * T
 
 
 def tile_attend_doubled_pl_kernel(tc, query, keys_words, keys_scales, gain, slot_factor, vals, offs, out_0, out_1, out_2):
     nc = tc.nc
     with ExitStack() as ctx:
         sb = ctx.enter_context(tc.tile_pool(name="sb", bufs=1))
+        shared = ctx.enter_context(tc.tile_pool(name="shared", bufs=1))
         ps = ctx.enter_context(tc.psum_pool(name="ps", bufs=1))
 
         q_raw = sb.tile([P, PACK, Q], F32, name="q_raw")
@@ -49,7 +51,7 @@ def tile_attend_doubled_pl_kernel(tc, query, keys_words, keys_scales, gain, slot
         nc.sync.dma_start(os_col[:], slot_factor.rearrange("o (p t) -> p (o t)", t=PACK))
 
         vals_rows = vals.rearrange("(p t) c -> t p c", t=PACK)
-        v_pool = [sb.tile([P, T], F32, name="v_pool%d" % t, tag="pool%d" % t, align_bytes=64) for t in range(PACK)]
+        v_pool = [shared.tile([P, T], F32, name="v_pool%d" % t, offset=t * POOL_BYTES) for t in range(PACK)]
         for t in range(PACK):
             nc.sync.dma_start(v_pool[t][:], vals_rows[t])
 
@@ -58,6 +60,8 @@ def tile_attend_doubled_pl_kernel(tc, query, keys_words, keys_scales, gain, slot
         os_rows = ps.tile([P, PACK, P], F32, name="os_rows")
         for t in range(PACK):
             nc.tensor.transpose(os_rows[:, t, :], os_col[:, t : t + 1].to_broadcast([P, P]), ident[:])
+        os_sb = sb.tile([P, I], F32, name="os_sb")
+        nc.scalar.copy(os_sb[:].rearrange("q (p t) -> q p t", t=PACK), os_rows[:].rearrange("q t p -> q p t"))
 
 
         q_bf = sb.tile([P, Q, PACK], BF16, name="q_bf", align_bytes=64)
@@ -109,9 +113,6 @@ def tile_attend_doubled_pl_kernel(tc, query, keys_words, keys_scales, gain, slot
             nc.vector.quantize_mx(codes.bitcast(FP8X4), scales[:], grouped[:])
             return codes, scales[:]
 
-        def codes_tile(name, count, tag):
-            return sb.tile([P, count * P], U32, name=name, tag=tag, align_bytes=64)
-
         def pick_values(t):
             picked = sb.tile([P, I], BF16, name="picked%d" % t, align_bytes=64)
             nc.vector.tensor_copy(picked[:], v_pool[t][:].indirect(offsets[:]))
@@ -127,78 +128,77 @@ def tile_attend_doubled_pl_kernel(tc, query, keys_words, keys_scales, gain, slot
             top.append(sb.tile([P, 2], F32, name="top%d" % h))
             nc.vector.memset(top[h][:, 0:1], -1.0)
         v_grouped = [pick_values(0)]
-        gained = sb.tile([P, HALVES * (I + 1)], F32, name="gained", tag="pool0", align_bytes=64)
+        neg_gain = sb.tile([P, HALVES], F32, name="neg_gain")
+        nc.scalar.activation(neg_gain[:], gain_col[:], ACT.Copy, scale=-float(I))
+        gained = shared.tile([P, HALVES * (I + 1)], F32, name="gained", offset=0)
         pu = [gained[:, h * I : (h + 1) * I] for h in range(HALVES)]
-        rz1 = [gained[:, HALVES * I + h : HALVES * I + h + 1] for h in range(HALVES)]
+        rz1 = gained[:, HALVES * I :]
+        nc.vector.reciprocal(rz1, z1[:])
         for h in range(HALVES):
-            nc.vector.tensor_scalar(pu[h], p1[h][:], gain_col[:, h : h + 1], None, ALU.mult, ALU.max, accum_out=top[h][:, 1:2])
-            if h == 0:
-                nc.vector.reciprocal(gained[:, HALVES * I :], z1[:])
+            nc.vector.tensor_scalar(pu[h], p1[h][:], neg_gain[:, h : h + 1], None, ALU.mult, ALU.min, accum_out=top[h][:, 1:2])
             bias2.append(sb.tile([P, 2], F32, name="bias2_%d" % h))
-            nc.vector.tensor_scalar(bias2[h][:], top[h][:], rz1[h], -float(I), ALU.mult, ALU.mult)
+            nc.scalar.activation(bias2[h][:], top[h][:], ACT.Copy, scale=rz1[:, h : h + 1])
             p2.append(sb.tile([P, I], F32, name="p2_%d" % h))
             z2.append(col("z2_%d" % h))
             nc.scalar.activation(p2[h][:], pu[h], ACT.Exp, bias=bias2[h][:, 1:2], scale=bias2[h][:, 0:1], accum_out=z2[h][:])
-        v_mx = [quantize(v_grouped[0], "v0", codes_tile("v0_codes", 1, "v0_codes")[:])]
         v_grouped.append(pick_values(1))
-        rz2 = sb.tile([P, HALVES], F32, name="rz2", tag="pool1", align_bytes=64)
+        rz2 = shared.tile([P, HALVES], F32, name="rz2", offset=POOL_BYTES)
+        w_bf = [sb.tile([P, I], BF16, name="w_bf%d" % h, align_bytes=64) for h in range(HALVES)]
         for h in range(HALVES):
             nc.vector.reciprocal(rz2[:, h : h + 1], z2[h][:])
+        weighted = sb.tile([P, I], F32, name="weighted")
+        nc.gpsimd.tensor_tensor(weighted[:], p2[0][:], os_sb[:], ALU.mult)
+        nc.vector.scalar_tensor_tensor(
+            w_bf[1][:].rearrange("q (p t) -> q p t", t=PACK),
+            p2[1][:].rearrange("q (p t) -> q p t", t=PACK),
+            rz2[:, 1:2],
+            os_rows[:].rearrange("q t p -> q p t"),
+            ALU.mult,
+            ALU.mult,
+        )
+        nc.scalar.activation(w_bf[0][:], weighted[:], ACT.Copy, scale=rz2[:, 0:1])
         for h in range(HALVES):
-            w_bf = sb.tile([P, I], BF16, name="w_bf%d" % h, align_bytes=64)
-            nc.vector.scalar_tensor_tensor(
-                w_bf[:].rearrange("q (p t) -> q p t", t=PACK),
-                p2[h][:].rearrange("q (p t) -> q p t", t=PACK),
-                rz2[:, h : h + 1],
-                os_rows[:].rearrange("q t p -> q p t"),
-                ALU.mult,
-                ALU.mult,
-            )
-            w_grouped.append(turn(w_bf, "w%d" % h, "half%d" % h, 1))
+            w_grouped.append(turn(w_bf[h], "w%d" % h, "half%d" % h, 1))
         v_grouped.append(pick_values(2))
-        mid_codes = codes_tile("mid_codes", 3, "pool2")
-        v_mx.append(quantize(v_grouped[1], "v1", mid_codes[:, 0:P]))
-        w_mx = [quantize(w_grouped[h], "w%d" % h, mid_codes[:, (h + 1) * P : (h + 2) * P]) for h in range(HALVES)]
+        v_grouped.append(pick_values(3))
+        late_codes = shared.tile([P, 5, P], U32, name="late_codes", offset=3 * POOL_BYTES, align_bytes=64)
+        w_mx = [quantize(w_grouped[0], "w0", late_codes[:, 0, :])]
+        v_mx = [quantize(v_grouped[t], "v%d" % t, late_codes[:, 1 + t, :]) for t in range(PACK - 1)]
+        w_mx.append(quantize(w_grouped[1], "w1", late_codes[:, 4, :]))
+        v3_codes = sb.tile([P, P], U32, name="v3_codes", align_bytes=64)
+        v_mx.append(quantize(v_grouped[3], "v3", v3_codes[:]))
 
         sums = [ps.tile([P, PACK, P], F32, name="sums%d" % h) for h in range(HALVES)]
         result = sb.tile([P, PACK, Q], F32, name="result")
         out_rows = out_0.rearrange("(p t) q -> p t q", t=PACK)
 
-        def products(t):
-            for h in range(HALVES):
-                nc.tensor.matmul_mx(
-                    sums[h][:, t, :],
-                    lhsT=v_mx[t][0].bitcast(FP8X4),
-                    lhsT_scale=v_mx[t][1],
-                    rhs=w_mx[h][0].bitcast(FP8X4),
-                    rhs_scale=w_mx[h][1],
-                    start=True,
-                    stop=True,
-                )
+        def product(t, h):
+            nc.tensor.matmul_mx(
+                sums[h][:, t, :],
+                lhsT=v_mx[t][0].bitcast(FP8X4),
+                lhsT_scale=v_mx[t][1],
+                rhs=w_mx[h][0].bitcast(FP8X4),
+                rhs_scale=w_mx[h][1],
+                start=True,
+                stop=True,
+            )
 
-        def hand_out(rows, h):
-            nc.scalar.copy(result[:, rows, h * P : (h + 1) * P], sums[h][:, rows, :])
-
-        products(0)
-        products(1)
+        last = PACK - 1
         for h in range(HALVES):
-            hand_out(slice(0, 2), h)
-        nc.sync.dma_start(out_rows[:, 0:2, :], result[:, 0:2, :])
-        v_grouped.append(pick_values(3))
-        v_mx.append(quantize(v_grouped[2], "v2", codes_tile("v2_codes", 1, "pool3")[:]))
-        products(2)
+            for t in range(last):
+                product(t, h)
+        nc.scalar.copy(result[:, 0:last, 0:P], sums[0][:, 0:last, :])
+        nc.vector.tensor_copy(result[:, 0:last, P:Q], sums[1][:, 0:last, :])
+        nc.sync.dma_start(out_rows[:, 0:last, :], result[:, 0:last, :])
         for h in range(HALVES):
-            hand_out(2, h)
-        nc.sync.dma_start(out_rows[:, 2, :], result[:, 2, :])
-        v_mx.append(quantize(v_grouped[3], "v3", codes_tile("v3_codes", 1, "v3_codes")[:]))
-        products(3)
+            product(last, h)
 
         y_bf = [sb.tile([P, P, PACK], BF16, name="y_bf%d" % h, align_bytes=64) for h in range(HALVES)]
         nc.scalar.copy(y_bf[0][:], sums[0][:].rearrange("p t q -> p q t"))
         nc.vector.tensor_copy(y_bf[1][:], sums[1][:].rearrange("p t q -> p q t"))
         for h in range(HALVES):
-            hand_out(3, h)
-        nc.scalar.dma_start(out_rows[:, 3, :], result[:, 3, :])
+            nc.scalar.copy(result[:, last, h * P : (h + 1) * P], sums[h][:, last, :])
+        nc.scalar.dma_start(out_rows[:, last, :], result[:, last, :])
         y_codes = sb.tile([P, Q], U32, name="y_codes", align_bytes=64)
         y_scales = sb.tile([P, Q], U8, name="y_scales", align_bytes=64)
         for h in range(HALVES):

from contextlib import ExitStack

import concourse.mybir as mybir
from concourse.masks import make_identity

D, E, T, I, Q = 512, 512, 2048, 512, 256
FLOPS = 2 * D * I * Q + 2 * I * E * Q

F32 = mybir.dt.float32
BF16 = mybir.dt.bfloat16
I32 = mybir.dt.int32
U32 = mybir.dt.uint32
U16 = mybir.dt.uint16
U8 = mybir.dt.uint8
FP8X4 = mybir.dt.float8_e4m3fn_x4
ALU = mybir.AluOpType
ACT = mybir.ActivationFunctionType
AXIS = mybir.AxisListType

P = 128
PACK = 4
HALVES = Q // P
POOL_BYTES = 4 * T


def tile_attend_doubled_pl_kernel(tc, query, keys_words, keys_scales, gain, slot_factor, vals, offs, out_0, out_1, out_2):
    nc = tc.nc
    with ExitStack() as ctx:
        sb = ctx.enter_context(tc.tile_pool(name="sb", bufs=1))
        shared = ctx.enter_context(tc.tile_pool(name="shared", bufs=1))
        ps = ctx.enter_context(tc.psum_pool(name="ps", bufs=1))

        q_raw = sb.tile([P, PACK, Q], F32, name="q_raw")
        nc.sync.dma_start(q_raw[:], query.rearrange("(p t) q -> p t q", t=PACK))
        offsets = sb.tile([P, I // 16], U16, name="offsets")
        nc.sync.dma_start(offsets[:], offs)

        key_bytes = sb.tile([P, T], U8, name="key_bytes", align_bytes=64)
        nc.gpsimd.memset(key_bytes[:].bitcast(I32), 0)
        for quad in range(4):
            nc.sync.dma_start(
                key_bytes[32 * quad : 32 * quad + 4, :].bitcast(I32),
                keys_scales[0, 4 * quad : 4 * quad + 4, :].bitcast(I32),
            )
        key_words = sb.tile([P, T], U32, name="key_words", align_bytes=64)
        nc.sync.dma_start(key_words[:].bitcast(I32), keys_words[0].rearrange("p n t -> p (n t)").bitcast(I32))
        gain_col = sb.tile([P, HALVES], F32, name="gain_col")
        with nc.allow_non_contiguous_dma(reason="one gain value to a partition"):
            nc.sync.dma_start(gain_col[:], gain.rearrange("(h p) o -> p (h o)", p=P))
        os_col = sb.tile([P, PACK], F32, name="os_col")
        nc.sync.dma_start(os_col[:], slot_factor.rearrange("o (p t) -> p (o t)", t=PACK))

        vals_rows = vals.rearrange("(p t) c -> t p c", t=PACK)
        v_pool = [shared.tile([P, T], F32, name="v_pool%d" % t, offset=t * POOL_BYTES) for t in range(PACK)]
        for t in range(PACK):
            nc.sync.dma_start(v_pool[t][:], vals_rows[t])

        ident = sb.tile([P, P], F32, name="ident")
        make_identity(nc, ident[:])
        os_rows = ps.tile([P, PACK, P], F32, name="os_rows")
        for t in range(PACK):
            nc.tensor.transpose(os_rows[:, t, :], os_col[:, t : t + 1].to_broadcast([P, P]), ident[:])
        os_sb = sb.tile([P, I], F32, name="os_sb")
        nc.scalar.copy(os_sb[:].rearrange("q (p t) -> q p t", t=PACK), os_rows[:].rearrange("q t p -> q p t"))


        q_bf = sb.tile([P, Q, PACK], BF16, name="q_bf", align_bytes=64)
        nc.vector.tensor_copy(
            q_bf[:].rearrange("p (c i) t -> p c t i", i=4),
            q_raw[:].rearrange("p t (c i) -> p c t i", i=4),
        )
        kg_bytes = sb.tile([P, I], U8, name="kg_bytes", align_bytes=64)
        nc.vector.tensor_copy(kg_bytes[:], key_bytes[:].indirect(offsets[:]))
        q_codes = sb.tile([P, Q], U32, name="q_codes", align_bytes=64)
        q_scales = sb.tile([P, Q], U8, name="q_scales", align_bytes=64)
        nc.vector.quantize_mx(q_codes[:].bitcast(FP8X4), q_scales[:], q_bf[:].rearrange("p q t -> p (q t)"))

        kg_words = sb.tile([P, I], U32, name="kg_words", align_bytes=64)
        scores = [ps.tile([P, I], F32, name="scores%d" % h, tag="half%d" % h) for h in range(HALVES)]
        for part in range(2):
            slots = slice(part * I // 2, (part + 1) * I // 2)
            entries = offsets[:, part * I // 32 : (part + 1) * I // 32]
            nc.vector.tensor_copy(kg_words[:, slots], key_words[:].indirect(entries))
            for h in range(HALVES):
                cols = slice(h * P, (h + 1) * P)
                nc.tensor.matmul_mx(
                    scores[h][:, slots],
                    lhsT=q_codes[:, cols].bitcast(FP8X4),
                    lhsT_scale=q_scales[:, cols],
                    rhs=kg_words[:, slots].bitcast(FP8X4),
                    rhs_scale=kg_bytes[:, slots],
                    start=True,
                    stop=True,
                )

        def col(name):
            return sb.tile([P, 1], F32, name=name)

        def turn(rows_bf, name, bank_tag, bank_bufs):
            turned = ps.tile([P, 2, P], F32, name=name + "_turned", tag=bank_tag, bufs=bank_bufs)
            words = rows_bf[:].bitcast(F32)
            for u in range(2):
                nc.tensor.transpose(turned[:, u, :], words[:, u : I // 2 : 2], ident[:])
            grouped = sb.tile([P, P * PACK], BF16, name=name + "_grouped", align_bytes=64)
            nc.scalar.copy(
                grouped[:].bitcast(F32).rearrange("p (m u) -> p m u", u=2),
                turned[:].rearrange("p u m -> p m u"),
            )
            return grouped

        def quantize(grouped, name, codes):
            scales = sb.tile([P, P], U8, name=name + "_scales", align_bytes=64)
            nc.vector.quantize_mx(codes.bitcast(FP8X4), scales[:], grouped[:])
            return codes, scales[:]

        def pick_values(t):
            picked = sb.tile([P, I], BF16, name="picked%d" % t, align_bytes=64)
            nc.vector.tensor_copy(picked[:], v_pool[t][:].indirect(offsets[:]))
            return turn(picked, "v%d" % t, "v_turned", 2)

        neg_max, p1, top, bias2, p2, z2, w_grouped = [[] for k in range(7)]
        z1 = sb.tile([P, HALVES], F32, name="z1")
        for h in range(HALVES):
            neg_max.append(col("neg_max%d" % h))
            nc.vector.tensor_reduce(neg_max[h][:], scores[h][:], AXIS.X, ALU.max, negate=True)
            p1.append(sb.tile([P, I], F32, name="p1_%d" % h))
            nc.scalar.activation(p1[h][:], scores[h][:], ACT.Exp, bias=neg_max[h][:], accum_out=z1[:, h : h + 1])
            top.append(sb.tile([P, 2], F32, name="top%d" % h))
            nc.vector.memset(top[h][:, 0:1], -1.0)
        v_grouped = [pick_values(0)]
        neg_gain = sb.tile([P, HALVES], F32, name="neg_gain")
        nc.scalar.activation(neg_gain[:], gain_col[:], ACT.Copy, scale=-float(I))
        gained = shared.tile([P, HALVES * (I + 1)], F32, name="gained", offset=0)
        pu = [gained[:, h * I : (h + 1) * I] for h in range(HALVES)]
        rz1 = gained[:, HALVES * I :]
        nc.vector.reciprocal(rz1, z1[:])
        for h in range(HALVES):
            nc.vector.tensor_scalar(pu[h], p1[h][:], neg_gain[:, h : h + 1], None, ALU.mult, ALU.min, accum_out=top[h][:, 1:2])
            bias2.append(sb.tile([P, 2], F32, name="bias2_%d" % h))
            nc.scalar.activation(bias2[h][:], top[h][:], ACT.Copy, scale=rz1[:, h : h + 1])
            p2.append(sb.tile([P, I], F32, name="p2_%d" % h))
            z2.append(col("z2_%d" % h))
            nc.scalar.activation(p2[h][:], pu[h], ACT.Exp, bias=bias2[h][:, 1:2], scale=bias2[h][:, 0:1], accum_out=z2[h][:])
        v_grouped.append(pick_values(1))
        rz2 = shared.tile([P, HALVES], F32, name="rz2", offset=POOL_BYTES)
        w_bf = [sb.tile([P, I], BF16, name="w_bf%d" % h, align_bytes=64) for h in range(HALVES)]
        for h in range(HALVES):
            nc.vector.reciprocal(rz2[:, h : h + 1], z2[h][:])
        weighted = sb.tile([P, I], F32, name="weighted")
        nc.gpsimd.tensor_tensor(weighted[:], p2[0][:], os_sb[:], ALU.mult)
        nc.vector.scalar_tensor_tensor(
            w_bf[1][:].rearrange("q (p t) -> q p t", t=PACK),
            p2[1][:].rearrange("q (p t) -> q p t", t=PACK),
            rz2[:, 1:2],
            os_rows[:].rearrange("q t p -> q p t"),
            ALU.mult,
            ALU.mult,
        )
        nc.scalar.activation(w_bf[0][:], weighted[:], ACT.Copy, scale=rz2[:, 0:1])
        for h in range(HALVES):
            w_grouped.append(turn(w_bf[h], "w%d" % h, "half%d" % h, 1))
        v_grouped.append(pick_values(2))
        v_grouped.append(pick_values(3))
        late_codes = shared.tile([P, 5, P], U32, name="late_codes", offset=3 * POOL_BYTES, align_bytes=64)
        w_mx = [quantize(w_grouped[0], "w0", late_codes[:, 0, :])]
        v_mx = [quantize(v_grouped[t], "v%d" % t, late_codes[:, 1 + t, :]) for t in range(PACK - 1)]
        w_mx.append(quantize(w_grouped[1], "w1", late_codes[:, 4, :]))
        v3_codes = sb.tile([P, P], U32, name="v3_codes", align_bytes=64)
        v_mx.append(quantize(v_grouped[3], "v3", v3_codes[:]))

        sums = [ps.tile([P, PACK, P], F32, name="sums%d" % h) for h in range(HALVES)]
        result = sb.tile([P, PACK, Q], F32, name="result")
        out_rows = out_0.rearrange("(p t) q -> p t q", t=PACK)

        def product(t, h):
            nc.tensor.matmul_mx(
                sums[h][:, t, :],
                lhsT=v_mx[t][0].bitcast(FP8X4),
                lhsT_scale=v_mx[t][1],
                rhs=w_mx[h][0].bitcast(FP8X4),
                rhs_scale=w_mx[h][1],
                start=True,
                stop=True,
            )

        last = PACK - 1
        for h in range(HALVES):
            for t in range(last):
                product(t, h)
        nc.scalar.copy(result[:, 0:last, 0:P], sums[0][:, 0:last, :])
        nc.vector.tensor_copy(result[:, 0:last, P:Q], sums[1][:, 0:last, :])
        nc.sync.dma_start(out_rows[:, 0:last, :], result[:, 0:last, :])
        for h in range(HALVES):
            product(last, h)

        y_bf = [sb.tile([P, P, PACK], BF16, name="y_bf%d" % h, align_bytes=64) for h in range(HALVES)]
        nc.scalar.copy(y_bf[0][:], sums[0][:].rearrange("p t q -> p q t"))
        nc.vector.tensor_copy(y_bf[1][:], sums[1][:].rearrange("p t q -> p q t"))
        for h in range(HALVES):
            nc.scalar.copy(result[:, last, h * P : (h + 1) * P], sums[h][:, last, :])
        nc.scalar.dma_start(out_rows[:, last, :], result[:, last, :])
        y_codes = sb.tile([P, Q], U32, name="y_codes", align_bytes=64)
        y_scales = sb.tile([P, Q], U8, name="y_scales", align_bytes=64)
        for h in range(HALVES):
            cols = slice(h * P, (h + 1) * P)
            nc.vector.quantize_mx(
                y_codes[:, cols].bitcast(FP8X4), y_scales[:, cols], y_bf[h][:].rearrange("p q t -> p (q t)")
            )
        nc.sync.dma_start(out_1[0].rearrange("p n t -> p (n t)").bitcast(I32), y_codes[:].bitcast(I32))
        for quad in range(4):
            queue = nc.sync if quad < 2 else nc.scalar
            queue.dma_start(
                out_2[0, 4 * quad : 4 * quad + 4, :].bitcast(I32),
                y_scales[32 * quad : 32 * quad + 4, :].bitcast(I32),
            )
